import numpy as np
import ml_dtypes


def mxq(x, axis, fmt="e4m3"):
    dtype, down = {"e4m3": (ml_dtypes.float8_e4m3fn, 7), "e5m2": (ml_dtypes.float8_e5m2, 14)}[fmt]
    v = np.moveaxis(np.asarray(x, np.float32).astype(ml_dtypes.bfloat16).astype(np.float64), axis, -1)
    blocks = v.reshape(v.shape[:-1] + (-1, 32))
    amax = np.abs(blocks).max(-1, keepdims=True)
    byte = np.maximum(np.where(amax > 0, np.frexp(amax)[1] - 1 + 127, 0) - down, 1)
    scale = np.exp2(byte - 127.0)
    codes = (blocks / scale).astype(np.float32).astype(dtype).astype(np.float64)
    return np.moveaxis((codes * scale).reshape(v.shape), -1, axis)


WIDE = False


def mx_kscale(k):
    if not WIDE:
        return np.ones(k)
    levels = np.array([10, -10, 5, -5, 0])
    if k % 512:
        return np.exp2(np.random.permutation(np.resize(levels, k // 32))).repeat(32)
    a = np.empty((k // 512, 16))
    for p in range(k // 512):
        a[p, :8] = np.random.permutation(np.resize(levels, 8))
        for g in range(8):
            far = levels[np.abs(levels - a[p, g]) >= 10]
            a[p, g + 8] = far[np.random.randint(len(far))]
    return np.exp2(a.ravel()).repeat(32)


def f64(x):
    return np.asarray(x).astype(np.float64)


def striped(idx):
    return np.tile(idx.reshape(-1, 16).T, (8, 1)).astype(np.uint16)


def unstriped(offs):
    return offs[:16].T.reshape(-1).astype(np.int64)


E2M1 = np.array([0.0, 0.5, 1.0, 1.5, 2.0, 3.0, 4.0, 6.0, -0.0, -0.5, -1.0, -1.5, -2.0, -3.0, -4.0, -6.0])


def pack_weight(w, fmt):
    k, n = w.shape
    w = f64(np.asarray(w, np.float32).astype(ml_dtypes.bfloat16)).reshape(k // 32, 32, n)
    amax = np.abs(w).max(1)
    if fmt == "e4m3":
        byte = np.frexp(amax)[1] - 1 + 127 - 7
    else:
        mant, ex = np.frexp(amax / 6.0)
        byte = np.where(mant > 0.5, ex, ex - 1) + 127
    byte = np.clip(np.where(amax > 0, byte, 1), 1, 254)
    scaled = (w * np.exp2(127.0 - byte)[:, None, :]).reshape(k, n).astype(np.float32)
    by_word = np.ascontiguousarray(scaled.reshape(k // 512, 128, 4, n).transpose(0, 1, 3, 2))
    if fmt == "e4m3":
        words = by_word.astype(ml_dtypes.float8_e4m3fn).view(np.uint8)
    else:
        c = by_word.astype(ml_dtypes.float4_e2m1fn).view(np.uint8) & 0xF
        words = (c[..., 0::2] | (c[..., 1::2] << 4)).reshape(k // 512, 128, 2 * n)
    return np.ascontiguousarray(words), np.ascontiguousarray(byte.astype(np.uint8).reshape(k // 512, 16, n))


def unpack_weight(words, scales, fmt):
    g, _, n = scales.shape
    words = np.ascontiguousarray(words).reshape(g, 128, n, -1)
    if fmt == "e4m3":
        vals = words.view(ml_dtypes.float8_e4m3fn).astype(np.float64)
    else:
        nib = np.empty((g, 128, n, 4), np.uint8)
        nib[..., 0::2] = words & 0xF
        nib[..., 1::2] = words >> 4
        vals = E2M1[nib]
    vals = vals * np.repeat(np.exp2(scales.astype(np.float64) - 127.0), 8, axis=1)[..., None]
    return vals.transpose(0, 1, 3, 2).reshape(g * 512, n)


def pack_table(v):
    words, scales = pack_weight(v, "e4m3")
    return np.concatenate([words.reshape(words.shape[0], -1), scales.reshape(scales.shape[0], -1)], axis=1)


def unpack_table(tab):
    g, t = tab.shape[0], tab.shape[1] // 528
    return unpack_weight(tab[:, :512 * t].reshape(g, 128, t, 4), tab[:, 512 * t:].reshape(g, 16, t), "e4m3")


def split(x):
    m, e = np.frexp(f64(x))
    hi = np.ldexp(np.trunc(16.0 * m) / 16.0, e)
    return hi, f64(x) - hi


def silu(v):
    return v / (1.0 + np.exp(-np.maximum(v, -700.0)))


K, M, T, S = 2048, 512, 4096, 2048


def setup_inputs():
    n = np.random.standard_normal
    s = mx_kscale(K)[:, None]
    return {
        "tab": pack_table(n((K, T)) * s),
        "w": (n((K, M)) / np.sqrt(K) / s).astype(np.float32),
        "b": (0.3 * n(512)).astype(np.float32),
        "offs": striped(np.random.permutation(T)[:S]),
    }


def reference(tab, w, b, offs):
    tab_ = unpack_table(tab)[:, unstriped(offs)]
    w_hi, w_lo = split(w)
    w_hi_, w_lo_ = mxq(w_hi, 0, "e4m3"), mxq(w_lo, 0, "e4m3")
    y = w_hi_.T @ tab_ + w_lo_.T @ tab_
    return silu(y + f64(b)[:, None])

@@ -1,0 +1,214 @@
+from contextlib import ExitStack
+
+import concourse.mybir as mybir
+
+K, M, T, S = 2048, 512, 4096, 2048
+FLOPS = 2 * 2 * K * M * S
+
+F32 = mybir.dt.float32
+BF16 = mybir.dt.bfloat16
+I32 = mybir.dt.int32
+U32 = mybir.dt.uint32
+U16 = mybir.dt.uint16
+U8 = mybir.dt.uint8
+FP8X4 = mybir.dt.float8_e4m3fn_x4
+
+P = 128
+PACK = 4
+K_PASS = P * PACK
+PASSES = K // K_PASS
+M_TILE = 128
+M_TILES_HALF = 2
+HALF = M_TILES_HALF * M_TILE
+N_TILE = 512
+N_TILES = S // N_TILE
+BANKS = 8
+LIST_ROWS = 16
+ALIGN = 64
+
+HI_MASK = 0xFFF0FFF0 - 2**32
+
+SPLIT = 2560
+
+RUN = 4
+
+
+def tile_list_tabw_hl_silu_kernel(tc, tab, w, b, offs, out):
+    nc = tc.nc
+    silu = mybir.ActivationFunctionType.Silu
+    bitwise_and = mybir.AluOpType.bitwise_and
+    subtract = mybir.AluOpType.subtract
+
+    with ExitStack() as ctx:
+        keep = ctx.enter_context(tc.tile_pool(name="keep", bufs=1))
+        stage = ctx.enter_context(tc.tile_pool(name="stage", bufs=PASSES))
+        outs = ctx.enter_context(tc.tile_pool(name="outs", bufs=BANKS))
+        psum = ctx.enter_context(tc.psum_pool(name="psum", bufs=BANKS))
+
+        offsets = keep.tile([P, S // LIST_ROWS], U16, name="offsets")
+        nc.sync.dma_start(offsets[:], offs)
+
+        planes = keep.tile([P, T // 4], I32, name="planes", align_bytes=ALIGN)
+        nc.vector.memset(planes[:], 0)
+
+        warm = keep.tile([P, 1], F32, name="warm")
+        nc.gpsimd.memset(warm[:], 0.0)
+        nc.scalar.activation(out=warm[:], in_=warm[:], func=silu)
+
+        words = [keep.tile([P, T], I32, name="words%d" % a, align_bytes=ALIGN) for a in range(PASSES)]
+        raws = {}
+        for half in range(2):
+            for a in range(PASSES):
+                raws[(half, a)] = keep.tile([P, PACK, HALF], F32, name="raw_%d_%d" % (half, a), align_bytes=ALIGN)
+        bias = keep.tile([P, M // M_TILE], F32, name="bias")
+
+        def load_weights(half, a):
+            rows = w[a * K_PASS : (a + 1) * K_PASS, half * HALF : (half + 1) * HALF]
+            nc.sync.dma_start(out=raws[(half, a)][:], in_=rows.rearrange("(p j) n -> p j n", j=PACK))
+
+        def load_words(a, cols):
+            rows = tab[a, 0 : K_PASS * T].rearrange("(p t) -> p t", p=P).bitcast(I32)
+            nc.sync.dma_start(out=words[a][:, cols], in_=rows[:, cols])
+
+        load_weights(0, 0)
+
+        for quadrant in range(4):
+            first = K_PASS * T + 4 * quadrant * T
+            rows = tab[:, first : first + 4 * T].rearrange("a (r t) -> a r t", r=4).bitcast(I32)
+            nc.sync.dma_start(out=planes[32 * quadrant : 32 * quadrant + 16, :], in_=rows)
+
+        for a in range(PASSES):
+            load_words(a, slice(0, SPLIT))
+            if a < PASSES - 1:
+                load_weights(0, a + 1)
+            else:
+                load_weights(1, 0)
+            load_words(a, slice(SPLIT, T))
+            if a == PASSES - 2:
+                with nc.allow_non_contiguous_dma(reason="512 bias values, one to a partition"):
+                    nc.sync.dma_start(out=bias[:], in_=b.rearrange("(m p) -> p m", p=P))
+        for a in range(1, PASSES):
+            load_weights(1, a)
+
+        interleaved = "p (c i j) -> p c j i"
+        parts = {}
+        codes = {}
+
+        def split(half, a, engine):
+            raw = raws[(half, a)]
+            upper = stage.tile([P, HALF * PACK], BF16, name="upper", align_bytes=ALIGN)
+            sixteens = raw[:].rearrange("p j n -> p (j n)").bitcast(BF16)
+            sixteens = sixteens.rearrange("p (j c i e) -> p c j i e", j=PACK, i=RUN, e=2)
+            nc.scalar.copy(out=upper[:].rearrange(interleaved, j=PACK, i=RUN), in_=sixteens[:, :, :, :, 1])
+            part = stage.tile([P, 2, HALF * PACK], BF16, name="part", align_bytes=ALIGN)
+            nc.vector.tensor_scalar(
+                out=part[:, 0].bitcast(I32),
+                in0=upper[:].bitcast(I32),
+                scalar1=HI_MASK,
+                scalar2=None,
+                op0=bitwise_and,
+            )
+            engine.tensor_tensor(
+                out=part[:, 1].rearrange(interleaved, j=PACK, i=RUN),
+                in0=raw[:].rearrange("p j (c i) -> p c j i", i=RUN),
+                in1=part[:, 0].rearrange(interleaved, j=PACK, i=RUN),
+                op=subtract,
+            )
+            parts[(half, a)] = part
+
+        def quantize(half, a):
+            code = keep.tile([P, 2 * HALF], U32, name="code_%d_%d" % (half, a), align_bytes=ALIGN)
+            scale = keep.tile([P, 2 * HALF], U8, name="scale_%d_%d" % (half, a), align_bytes=ALIGN)
+            nc.vector.quantize_mx(
+                out=code[:].bitcast(FP8X4),
+                scales=scale[:],
+                in_=parts[(half, a)][:].rearrange("p s e -> p (s e)"),
+            )
+            codes[(half, a)] = (code, scale)
+
+        picked_planes = keep.tile([P, S], U8, name="picked_planes", align_bytes=ALIGN)
+        picked = [keep.tile([P, S], U32, name="picked%d" % a, align_bytes=ALIGN) for a in range(PASSES)]
+
+        def list_part(first, count):
+            return offsets[:, first // LIST_ROWS : (first + count) // LIST_ROWS]
+
+        def gather_scales(first, count):
+            nc.vector.tensor_copy(
+                out=picked_planes[:, first : first + count],
+                in_=planes[:].bitcast(U8).indirect(list_part(first, count)),
+            )
+
+        def gather_words(a, first, count):
+            nc.vector.tensor_copy(
+                out=picked[a][:, first : first + count],
+                in_=words[a][:].bitcast(U32).indirect(list_part(first, count)),
+            )
+
+        sums = {}
+
+        def multiply(m, n, a, part, left=0, width=N_TILE):
+            if (m, n) not in sums:
+                sums[(m, n)] = psum.tile([M_TILE, N_TILE], F32, name="acc")
+            code, scale = codes[(m // M_TILES_HALF, a)]
+            first = part * HALF + (m % M_TILES_HALF) * M_TILE
+            channels = slice(first, first + M_TILE)
+            places = slice(n * N_TILE + left, n * N_TILE + left + width)
+            nc.tensor.matmul_mx(
+                out=sums[(m, n)][:, left : left + width],
+                lhsT=code[:, channels].bitcast(FP8X4),
+                lhsT_scale=scale[:, channels],
+                rhs=picked[a][:, places].bitcast(FP8X4),
+                rhs_scale=picked_planes[4 * a : P, places],
+                start=(a == 0 and part == 0),
+                stop=(a == PASSES - 1 and part == 1),
+            )
+
+        def finish(m, n, left=0, width=N_TILE):
+            done = outs.tile([M_TILE, width], F32, name="done")
+            nc.scalar.activation(out=done[:], in_=sums[(m, n)][:, left : left + width], func=silu, bias=bias[:, m : m + 1])
+            rows = slice(m * M_TILE, (m + 1) * M_TILE)
+            nc.sync.dma_start(out=out[rows, n * N_TILE + left : n * N_TILE + left + width], in_=done[:])
+
+        split(0, 0, nc.gpsimd)
+        for n in range(N_TILES):
+            gather_scales(n * N_TILE, N_TILE)
+        quantize(0, 0)
+        for a in range(PASSES - 1):
+            split(0, a + 1, nc.gpsimd)
+            gather_words(a, 0, S // 2)
+            gather_words(a, S // 2, S // 2)
+            quantize(0, a + 1)
+            for n in range(N_TILES):
+                for part in range(2):
+                    for m in range(M_TILES_HALF):
+                        multiply(m, n, a, part)
+        split(1, 0, nc.gpsimd)
+        for n in range(N_TILES):
+            gather_words(PASSES - 1, n * N_TILE, N_TILE)
+            for part in range(2):
+                for m in range(M_TILES_HALF):
+                    multiply(m, n, PASSES - 1, part)
+            for m in range(M_TILES_HALF):
+                finish(m, n)
+
+        quantize(1, 0)
+        for a in range(1, PASSES):
+            split(1, a, nc.vector)
+            quantize(1, a)
+        banks = [(m, n) for m in range(M_TILES_HALF, 2 * M_TILES_HALF) for n in range(N_TILES)]
+        second, last = banks[:-1], banks[-1]
+        early = PASSES // 2
+        for a in range(early):
+            for part in range(2):
+                for m, n in second:
+                    multiply(m, n, a, part)
+        for m, n in second:
+            for a in range(early, PASSES):
+                for part in range(2):
+                    multiply(m, n, a, part)
+            finish(m, n)
+        for left in range(0, N_TILE, N_TILE // 2):
+            for a in range(PASSES):
+                for part in range(2):
+                    multiply(*last, a, part, left, N_TILE // 2)
+            finish(*last, left, N_TILE // 2)

@@ -18,6 +18,7 @@ PACK = 4
 K_PASS = P * PACK
 PASSES = K // K_PASS
 M_TILE = 128
+M_TILES = M // M_TILE
 M_TILES_HALF = 2
 HALF = M_TILES_HALF * M_TILE
 N_TILE = 512
@@ -25,12 +26,10 @@ N_TILES = S // N_TILE
 BANKS = 8
 LIST_ROWS = 16
 ALIGN = 64
-
 HI_MASK = 0xFFF0FFF0 - 2**32
-
-SPLIT = 2560
-
 RUN = 4
+SPLIT = 1280
+EARLY = 3
 
 
 def tile_list_tabw_hl_silu_kernel(tc, tab, w, b, offs, out):
@@ -41,9 +40,9 @@ def tile_list_tabw_hl_silu_kernel(tc, tab, w, b, offs, out):
 
     with ExitStack() as ctx:
         keep = ctx.enter_context(tc.tile_pool(name="keep", bufs=1))
-        stage = ctx.enter_context(tc.tile_pool(name="stage", bufs=PASSES))
+        stage = ctx.enter_context(tc.tile_pool(name="stage", bufs=4))
         outs = ctx.enter_context(tc.tile_pool(name="outs", bufs=BANKS))
-        psum = ctx.enter_context(tc.psum_pool(name="psum", bufs=BANKS))
+        psum = ctx.enter_context(tc.psum_pool(name="psum", bufs=1))
 
         offsets = keep.tile([P, S // LIST_ROWS], U16, name="offsets")
         nc.sync.dma_start(offsets[:], offs)
@@ -57,158 +56,196 @@ def tile_list_tabw_hl_silu_kernel(tc, tab, w, b, offs, out):
 
         words = [keep.tile([P, T], I32, name="words%d" % a, align_bytes=ALIGN) for a in range(PASSES)]
         raws = {}
-        for half in range(2):
-            for a in range(PASSES):
-                raws[(half, a)] = keep.tile([P, PACK, HALF], F32, name="raw_%d_%d" % (half, a), align_bytes=ALIGN)
-        bias = keep.tile([P, M // M_TILE], F32, name="bias")
+        bias = keep.tile([P, M_TILES], F32, name="bias")
 
-        def load_weights(half, a):
-            rows = w[a * K_PASS : (a + 1) * K_PASS, half * HALF : (half + 1) * HALF]
-            nc.sync.dma_start(out=raws[(half, a)][:], in_=rows.rearrange("(p j) n -> p j n", j=PACK))
+        def load_weights(a, first, count):
+            raw = keep.tile([P, PACK, count * M_TILE], F32, name="raw_%d_%d" % (a, first), align_bytes=ALIGN)
+            rows = w[a * K_PASS : (a + 1) * K_PASS, first * M_TILE : (first + count) * M_TILE]
+            nc.sync.dma_start(out=raw[:], in_=rows.rearrange("(p j) n -> p j n", j=PACK))
+            raws[(a, first)] = (raw, count)
 
         def load_words(a, cols):
             rows = tab[a, 0 : K_PASS * T].rearrange("(p t) -> p t", p=P).bitcast(I32)
             nc.sync.dma_start(out=words[a][:, cols], in_=rows[:, cols])
 
-        load_weights(0, 0)
-
+        last = PASSES - 1
+        load_weights(0, 0, 2)
+        load_weights(0, 2, 1)
         for quadrant in range(4):
             first = K_PASS * T + 4 * quadrant * T
             rows = tab[:, first : first + 4 * T].rearrange("a (r t) -> a r t", r=4).bitcast(I32)
             nc.sync.dma_start(out=planes[32 * quadrant : 32 * quadrant + 16, :], in_=rows)
-
-        for a in range(PASSES):
+        for a in range(last):
             load_words(a, slice(0, SPLIT))
-            if a < PASSES - 1:
-                load_weights(0, a + 1)
-            else:
-                load_weights(1, 0)
+            load_weights(a + 1, 0, EARLY if a + 1 < last else EARLY - 1)
             load_words(a, slice(SPLIT, T))
-            if a == PASSES - 2:
-                with nc.allow_non_contiguous_dma(reason="512 bias values, one to a partition"):
-                    nc.sync.dma_start(out=bias[:], in_=b.rearrange("(m p) -> p m", p=P))
-        for a in range(1, PASSES):
-            load_weights(1, a)
+        load_words(last, slice(0, T))
+        with nc.allow_non_contiguous_dma(reason="512 bias values, one to a partition"):
+            nc.sync.dma_start(out=bias[:], in_=b.rearrange("(m p) -> p m", p=P))
+        load_weights(last, EARLY - 1, 2)
+        for a in range(last):
+            load_weights(a, EARLY, 1)
 
         interleaved = "p (c i j) -> p c j i"
+        WIDE = M_TILE * PACK
         parts = {}
         codes = {}
 
-        def split(half, a, engine):
-            raw = raws[(half, a)]
-            upper = stage.tile([P, HALF * PACK], BF16, name="upper", align_bytes=ALIGN)
+        def interleave(a, first, pool, name):
+            raw, count = raws[(a, first)]
+            upper = pool.tile([P, count * WIDE], BF16, name=name, align_bytes=ALIGN)
             sixteens = raw[:].rearrange("p j n -> p (j n)").bitcast(BF16)
             sixteens = sixteens.rearrange("p (j c i e) -> p c j i e", j=PACK, i=RUN, e=2)
             nc.scalar.copy(out=upper[:].rearrange(interleaved, j=PACK, i=RUN), in_=sixteens[:, :, :, :, 1])
-            part = stage.tile([P, 2, HALF * PACK], BF16, name="part", align_bytes=ALIGN)
+            return upper
+
+        def mask(a, first, upper, start, count):
+            part = stage.tile([P, 2, count * WIDE], BF16, name="part%d" % count, align_bytes=ALIGN)
             nc.vector.tensor_scalar(
                 out=part[:, 0].bitcast(I32),
-                in0=upper[:].bitcast(I32),
+                in0=upper[:, start * WIDE : (start + count) * WIDE].bitcast(I32),
                 scalar1=HI_MASK,
                 scalar2=None,
                 op0=bitwise_and,
             )
+            parts[(a, first + start)] = (part, raws[(a, first)][0][:, :, start * M_TILE : (start + count) * M_TILE], count)
+
+        def subtract_hi(a, m, engine):
+            part, raw, count = parts[(a, m)]
             engine.tensor_tensor(
                 out=part[:, 1].rearrange(interleaved, j=PACK, i=RUN),
-                in0=raw[:].rearrange("p j (c i) -> p c j i", i=RUN),
+                in0=raw.rearrange("p j (c i) -> p c j i", i=RUN),
                 in1=part[:, 0].rearrange(interleaved, j=PACK, i=RUN),
                 op=subtract,
             )
-            parts[(half, a)] = part
 
-        def quantize(half, a):
-            code = keep.tile([P, 2 * HALF], U32, name="code_%d_%d" % (half, a), align_bytes=ALIGN)
-            scale = keep.tile([P, 2 * HALF], U8, name="scale_%d_%d" % (half, a), align_bytes=ALIGN)
-            nc.vector.quantize_mx(
-                out=code[:].bitcast(FP8X4),
-                scales=scale[:],
-                in_=parts[(half, a)][:].rearrange("p s e -> p (s e)"),
-            )
-            codes[(half, a)] = (code, scale)
+        def subtract_woven(a, m):
+            part, raw, count = parts[(a, m)]
+            woven = stage.tile([P, count * WIDE], F32, name="woven%d" % count, align_bytes=ALIGN, bufs=2)
+            nc.scalar.copy(out=woven[:].rearrange("p (n j) -> p n j", j=PACK), in_=raw.rearrange("p j n -> p n j"))
+            nc.gpsimd.tensor_tensor(out=part[:, 1], in0=woven[:], in1=part[:, 0], op=subtract)
 
-        picked_planes = keep.tile([P, S], U8, name="picked_planes", align_bytes=ALIGN)
-        picked = [keep.tile([P, S], U32, name="picked%d" % a, align_bytes=ALIGN) for a in range(PASSES)]
+        def quantize(a, m):
+            part, raw, count = parts[(a, m)]
+            width = 2 * count * M_TILE
+            code = keep.tile([P, width], U32, name="code_%d_%d" % (a, m), align_bytes=ALIGN)
+            scale = keep.tile([P, width], U8, name="scale_%d_%d" % (a, m), align_bytes=ALIGN)
+            nc.vector.quantize_mx(out=code[:].bitcast(FP8X4), scales=scale[:], in_=part[:].rearrange("p s e -> p (s e)"))
+            for half in range(2):
+                for g in range(count):
+                    codes[(a, m + g, half)] = (code, scale, (half * count + g) * M_TILE)
 
-        def list_part(first, count):
-            return offsets[:, first // LIST_ROWS : (first + count) // LIST_ROWS]
+        def quantize_part(a, m, count, half, values):
+            width = count * M_TILE
+            code = keep.tile([P, width], U32, name="late_code%d" % half, align_bytes=ALIGN)
+            scale = keep.tile([P, width], U8, name="late_scale%d" % half, align_bytes=ALIGN)
+            nc.vector.quantize_mx(out=code[:].bitcast(FP8X4), scales=scale[:], in_=values)
+            for g in range(count):
+                codes[(a, m + g, half)] = (code, scale, g * M_TILE)
 
-        def gather_scales(first, count):
-            nc.vector.tensor_copy(
-                out=picked_planes[:, first : first + count],
-                in_=planes[:].bitcast(U8).indirect(list_part(first, count)),
-            )
+        picked_planes = {}
+        picked = {}
 
-        def gather_words(a, first, count):
-            nc.vector.tensor_copy(
-                out=picked[a][:, first : first + count],
-                in_=words[a][:].bitcast(U32).indirect(list_part(first, count)),
-            )
+        def list_part(n):
+            return offsets[:, n * N_TILE // LIST_ROWS : (n + 1) * N_TILE // LIST_ROWS]
+
+        def gather_scales(n, name):
+            picked_planes[n] = keep.tile([P, N_TILE], U8, name=name, align_bytes=ALIGN)
+            nc.vector.tensor_copy(out=picked_planes[n][:], in_=planes[:].bitcast(U8).indirect(list_part(n)))
+
+        def gather_words(a, n, name):
+            picked[(a, n)] = keep.tile([P, N_TILE], U32, name=name, align_bytes=ALIGN)
+            nc.vector.tensor_copy(out=picked[(a, n)][:], in_=words[a][:].bitcast(U32).indirect(list_part(n)))
 
         sums = {}
+        bank_of = list(range(BANKS)) + [0, 1, 3, 4, 6, 7, 2, 5, 0]
 
-        def multiply(m, n, a, part, left=0, width=N_TILE):
-            if (m, n) not in sums:
-                sums[(m, n)] = psum.tile([M_TILE, N_TILE], F32, name="acc")
-            code, scale = codes[(m // M_TILES_HALF, a)]
-            first = part * HALF + (m % M_TILES_HALF) * M_TILE
-            channels = slice(first, first + M_TILE)
-            places = slice(n * N_TILE + left, n * N_TILE + left + width)
-            nc.tensor.matmul_mx(
-                out=sums[(m, n)][:, left : left + width],
-                lhsT=code[:, channels].bitcast(FP8X4),
-                lhsT_scale=scale[:, channels],
-                rhs=picked[a][:, places].bitcast(FP8X4),
-                rhs_scale=picked_planes[4 * a : P, places],
-                start=(a == 0 and part == 0),
-                stop=(a == PASSES - 1 and part == 1),
-            )
+        def multiply(m, n, a, order, left=0, width=N_TILE, which=(0, 1)):
+            if (m, n, left) not in sums:
+                sums[(m, n, left)] = psum.tile([M_TILE, width], F32, name="acc%d" % bank_of[len(sums)])
+            for part in which:
+                code, scale, first = codes[(a, m, part)]
+                channels = slice(first, first + M_TILE)
+                nc.tensor.matmul_mx(
+                    out=sums[(m, n, left)][:],
+                    lhsT=code[:, channels].bitcast(FP8X4),
+                    lhsT_scale=scale[:, channels],
+                    rhs=picked[(a, n)][:, left : left + width].bitcast(FP8X4),
+                    rhs_scale=picked_planes[n][4 * a : P, left : left + width],
+                    start=(a == order[0] and part == 0),
+                    stop=(a == order[-1] and part == 1),
+                )
+            if a == order[-1] and which[-1] == 1:
+                done = outs.tile([M_TILE, width], F32, name="done")
+                nc.scalar.activation(out=done[:], in_=sums[(m, n, left)][:], func=silu, bias=bias[:, m : m + 1])
+                rows = slice(m * M_TILE, (m + 1) * M_TILE)
+                nc.sync.dma_start(out=out[rows, n * N_TILE + left : n * N_TILE + left + width], in_=done[:])
 
-        def finish(m, n, left=0, width=N_TILE):
-            done = outs.tile([M_TILE, width], F32, name="done")
-            nc.scalar.activation(out=done[:], in_=sums[(m, n)][:, left : left + width], func=silu, bias=bias[:, m : m + 1])
-            rows = slice(m * M_TILE, (m + 1) * M_TILE)
-            nc.sync.dma_start(out=out[rows, n * N_TILE + left : n * N_TILE + left + width], in_=done[:])
+        upward = list(range(PASSES))
+        first_sums = [(m, n) for n in range(EARLY) for m in range(EARLY)][:BANKS]
 
-        split(0, 0, nc.gpsimd)
-        for n in range(N_TILES):
-            gather_scales(n * N_TILE, N_TILE)
+        mask(0, 0, interleave(0, 0, stage, "upper"), 0, 2)
+        mask(0, 2, interleave(0, 2, stage, "upper"), 0, 1)
+        subtract_woven(0, 0)
+        subtract_woven(0, 2)
+        for n in range(EARLY):
+            gather_scales(n, "picked_planes%d" % n)
         quantize(0, 0)
-        for a in range(PASSES - 1):
-            split(0, a + 1, nc.gpsimd)
-            gather_words(a, 0, S // 2)
-            gather_words(a, S // 2, S // 2)
-            quantize(0, a + 1)
-            for n in range(N_TILES):
-                for part in range(2):
-                    for m in range(M_TILES_HALF):
-                        multiply(m, n, a, part)
-        split(1, 0, nc.gpsimd)
+        quantize(0, 2)
+        for a in range(last):
+            upper = interleave(a + 1, 0, stage, "upper")
+            mask(a + 1, 0, upper, 0, 2)
+            if a + 1 < last:
+                mask(a + 1, 0, upper, 2, 1)
+            subtract_woven(a + 1, 0)
+            if a + 1 < last:
+                subtract_woven(a + 1, 2)
+            for n in range(EARLY):
+                gather_words(a, n, "picked_%d_%d" % (a, n))
+            quantize(a + 1, 0)
+            if a + 1 < last:
+                quantize(a + 1, 2)
+            for m, n in first_sums:
+                multiply(m, n, a, upward)
         for n in range(N_TILES):
-            gather_words(PASSES - 1, n * N_TILE, N_TILE)
-            for part in range(2):
-                for m in range(M_TILES_HALF):
-                    multiply(m, n, PASSES - 1, part)
-            for m in range(M_TILES_HALF):
-                finish(m, n)
-
-        quantize(1, 0)
-        for a in range(1, PASSES):
-            split(1, a, nc.vector)
-            quantize(1, a)
-        banks = [(m, n) for m in range(M_TILES_HALF, 2 * M_TILES_HALF) for n in range(N_TILES)]
-        second, last = banks[:-1], banks[-1]
-        early = PASSES // 2
-        for a in range(early):
-            for part in range(2):
-                for m, n in second:
-                    multiply(m, n, a, part)
-        for m, n in second:
-            for a in range(early, PASSES):
-                for part in range(2):
-                    multiply(m, n, a, part)
-            finish(m, n)
+            gather_words(last, n, "picked_%d_%d" % (last, n))
+        upper = interleave(last, EARLY - 1, stage, "upper")
+        hi = keep.tile([P, 2 * WIDE], BF16, name="late_hi", align_bytes=ALIGN)
+        lo = keep.tile([P, 2 * WIDE], BF16, name="shared%d" % last, align_bytes=ALIGN)
+        nc.vector.tensor_scalar(
+            out=hi[:].bitcast(I32), in0=upper[:].bitcast(I32), scalar1=HI_MASK, scalar2=None, op0=bitwise_and
+        )
+        quantize_part(last, EARLY - 1, 2, 0, hi[:])
+        nc.vector.tensor_tensor(
+            out=lo[:].rearrange(interleaved, j=PACK, i=RUN),
+            in0=raws[(last, EARLY - 1)][0][:].rearrange("p j (c i) -> p c j i", i=RUN),
+            in1=hi[:].rearrange(interleaved, j=PACK, i=RUN),
+            op=subtract,
+        )
+        quantize_part(last, EARLY - 1, 2, 1, lo[:])
+        gather_scales(EARLY, "shared%d" % last)
+        for m, n in first_sums:
+            if m < EARLY - 1:
+                multiply(m, n, last, upward)
+        for a in range(last):
+            mask(a, EARLY, interleave(a, EARLY, keep, "shared%d" % a), 0, 1)
+            gather_words(a, EARLY, "shared%d" % a)
+            subtract_hi(a, EARLY, nc.vector)
+            quantize(a, EARLY)
+        for a in range(last):
+            multiply(EARLY - 1, EARLY - 1, a, upward)
+        turned = [last] + upward[:last]
+        for part in range(2):
+            for n in range(EARLY):
+                multiply(EARLY - 1, n, last, upward, which=(part,))
+            for n in range(EARLY):
+                multiply(EARLY, n, last, turned, which=(part,))
+        for a in turned:
+            for m in range(EARLY):
+                multiply(m, EARLY, a, turned)
+            if a != last:
+                for n in range(EARLY):
+                    multiply(EARLY, n, a, turned)
         for left in range(0, N_TILE, N_TILE // 2):
-            for a in range(PASSES):
-                for part in range(2):
-                    multiply(*last, a, part, left, N_TILE // 2)
-            finish(*last, left, N_TILE // 2)
+            for a in upward:
+                multiply(EARLY, EARLY, a, upward, left, N_TILE // 2)

@@ -50,10 +50,6 @@ def tile_list_tabw_hl_silu_kernel(tc, tab, w, b, offs, out):
         planes = keep.tile([P, T // 4], I32, name="planes", align_bytes=ALIGN)
         nc.vector.memset(planes[:], 0)
 
-        warm = keep.tile([P, 1], F32, name="warm")
-        nc.gpsimd.memset(warm[:], 0.0)
-        nc.scalar.activation(out=warm[:], in_=warm[:], func=silu)
-
         words = [keep.tile([P, T], I32, name="words%d" % a, align_bytes=ALIGN) for a in range(PASSES)]
         raws = {}
         bias = keep.tile([P, M_TILES], F32, name="bias")
@@ -71,10 +67,11 @@ def tile_list_tabw_hl_silu_kernel(tc, tab, w, b, offs, out):
         last = PASSES - 1
         load_weights(0, 0, 2)
         load_weights(0, 2, 1)
-        for quadrant in range(4):
+        for quadrant in (2, 3, 0, 1):
             first = K_PASS * T + 4 * quadrant * T
             rows = tab[:, first : first + 4 * T].rearrange("a (r t) -> a r t", r=4).bitcast(I32)
-            nc.sync.dma_start(out=planes[32 * quadrant : 32 * quadrant + 16, :], in_=rows)
+            for cols in (slice(0, T // 8), slice(T // 8, T // 4)):
+                nc.sync.dma_start(out=planes[32 * quadrant : 32 * quadrant + 16, cols], in_=rows[:, :, cols])
         for a in range(last):
             load_words(a, slice(0, SPLIT))
             load_weights(a + 1, 0, EARLY if a + 1 < last else EARLY - 1)
@@ -158,7 +155,7 @@ def tile_list_tabw_hl_silu_kernel(tc, tab, w, b, offs, out):
             nc.vector.tensor_copy(out=picked[(a, n)][:], in_=words[a][:].bitcast(U32).indirect(list_part(n)))
 
         sums = {}
-        bank_of = list(range(BANKS)) + [0, 1, 3, 4, 6, 7, 2, 5, 0]
+        bank_of = list(range(BANKS)) + [0, 1, 3, 4, 6, 7, 2, 5, 0, 6]
 
         def multiply(m, n, a, order, left=0, width=N_TILE, which=(0, 1)):
             if (m, n, left) not in sums:
@@ -179,7 +176,8 @@ def tile_list_tabw_hl_silu_kernel(tc, tab, w, b, offs, out):
                 done = outs.tile([M_TILE, width], F32, name="done")
                 nc.scalar.activation(out=done[:], in_=sums[(m, n, left)][:], func=silu, bias=bias[:, m : m + 1])
                 rows = slice(m * M_TILE, (m + 1) * M_TILE)
-                nc.sync.dma_start(out=out[rows, n * N_TILE + left : n * N_TILE + left + width], in_=done[:])
+                queue = nc.scalar if width < N_TILE // 2 and left + width == N_TILE else nc.sync
+                queue.dma_start(out=out[rows, n * N_TILE + left : n * N_TILE + left + width], in_=done[:])
 
         upward = list(range(PASSES))
         first_sums = [(m, n) for n in range(EARLY) for m in range(EARLY)][:BANKS]
@@ -246,6 +244,6 @@ def tile_list_tabw_hl_silu_kernel(tc, tab, w, b, offs, out):
             if a != last:
                 for n in range(EARLY):
                     multiply(EARLY, n, a, turned)
-        for left in range(0, N_TILE, N_TILE // 2):
+        for left, width in [(0, N_TILE // 2), (N_TILE // 2, N_TILE // 4), (3 * N_TILE // 4, N_TILE // 4)]:
             for a in upward:
-                multiply(EARLY, EARLY, a, upward, left, N_TILE // 2)
+                multiply(EARLY, EARLY, a, upward, left, width)

@@ -28,7 +28,7 @@ LIST_ROWS = 16
 ALIGN = 64
 HI_MASK = 0xFFF0FFF0 - 2**32
 RUN = 4
-SPLIT = 1280
+SPLIT = 1536
 EARLY = 3
 
 
@@ -74,12 +74,14 @@ def tile_list_tabw_hl_silu_kernel(tc, tab, w, b, offs, out):
                 nc.sync.dma_start(out=planes[32 * quadrant : 32 * quadrant + 16, cols], in_=rows[:, :, cols])
         for a in range(last):
             load_words(a, slice(0, SPLIT))
-            load_weights(a + 1, 0, EARLY if a + 1 < last else EARLY - 1)
+            load_weights(a + 1, 0, 2)
+            if a + 1 < last:
+                load_weights(a + 1, 2, 1)
             load_words(a, slice(SPLIT, T))
         load_words(last, slice(0, T))
+        load_weights(last, EARLY - 1, 2)
         with nc.allow_non_contiguous_dma(reason="512 bias values, one to a partition"):
             nc.sync.dma_start(out=bias[:], in_=b.rearrange("(m p) -> p m", p=P))
-        load_weights(last, EARLY - 1, 2)
         for a in range(last):
             load_weights(a, EARLY, 1)
 
@@ -191,10 +193,9 @@ def tile_list_tabw_hl_silu_kernel(tc, tab, w, b, offs, out):
         quantize(0, 0)
         quantize(0, 2)
         for a in range(last):
-            upper = interleave(a + 1, 0, stage, "upper")
-            mask(a + 1, 0, upper, 0, 2)
+            mask(a + 1, 0, interleave(a + 1, 0, stage, "upper"), 0, 2)
             if a + 1 < last:
-                mask(a + 1, 0, upper, 2, 1)
+                mask(a + 1, 2, interleave(a + 1, 2, stage, "upper"), 0, 1)
             subtract_woven(a + 1, 0)
             if a + 1 < last:
                 subtract_woven(a + 1, 2)

@@ -17,234 +17,219 @@ P = 128
 PACK = 4
 K_PASS = P * PACK
 PASSES = K // K_PASS
+LAST = PASSES - 1
 M_TILE = 128
 M_TILES = M // M_TILE
-M_TILES_HALF = 2
-HALF = M_TILES_HALF * M_TILE
 N_TILE = 512
+N_HALF = N_TILE // 2
 N_TILES = S // N_TILE
 BANKS = 8
 LIST_ROWS = 16
 ALIGN = 64
 HI_MASK = 0xFFF0FFF0 - 2**32
 RUN = 4
-SPLIT = 1536
 EARLY = 3
+WIDE = M_TILE * PACK
 
 
 def tile_list_tabw_hl_silu_kernel(tc, tab, w, b, offs, out):
     nc = tc.nc
     silu = mybir.ActivationFunctionType.Silu
-    bitwise_and = mybir.AluOpType.bitwise_and
-    subtract = mybir.AluOpType.subtract
+    interleaved = "p (c i j) -> p c j i"
 
     with ExitStack() as ctx:
         keep = ctx.enter_context(tc.tile_pool(name="keep", bufs=1))
-        stage = ctx.enter_context(tc.tile_pool(name="stage", bufs=4))
+        stage = ctx.enter_context(tc.tile_pool(name="stage", bufs=2))
         outs = ctx.enter_context(tc.tile_pool(name="outs", bufs=BANKS))
         psum = ctx.enter_context(tc.psum_pool(name="psum", bufs=1))
 
         offsets = keep.tile([P, S // LIST_ROWS], U16, name="offsets")
-        nc.sync.dma_start(offsets[:], offs)
-
         planes = keep.tile([P, T // 4], I32, name="planes", align_bytes=ALIGN)
-        nc.vector.memset(planes[:], 0)
-
         words = [keep.tile([P, T], I32, name="words%d" % a, align_bytes=ALIGN) for a in range(PASSES)]
-        raws = {}
         bias = keep.tile([P, M_TILES], F32, name="bias")
+        raws = {}
 
         def load_weights(a, first, count):
             raw = keep.tile([P, PACK, count * M_TILE], F32, name="raw_%d_%d" % (a, first), align_bytes=ALIGN)
             rows = w[a * K_PASS : (a + 1) * K_PASS, first * M_TILE : (first + count) * M_TILE]
             nc.sync.dma_start(out=raw[:], in_=rows.rearrange("(p j) n -> p j n", j=PACK))
-            raws[(a, first)] = (raw, count)
+            raws[(a, first)] = raw
 
-        def load_words(a, cols):
+        def load_words(a, cols=slice(0, T)):
             rows = tab[a, 0 : K_PASS * T].rearrange("(p t) -> p t", p=P).bitcast(I32)
             nc.sync.dma_start(out=words[a][:, cols], in_=rows[:, cols])
 
-        last = PASSES - 1
-        load_weights(0, 0, 2)
-        load_weights(0, 2, 1)
+        nc.sync.dma_start(offsets[:], offs)
+        nc.vector.memset(planes[:], 0)
+        load_weights(0, 0, EARLY)
         for quadrant in (2, 3, 0, 1):
             first = K_PASS * T + 4 * quadrant * T
             rows = tab[:, first : first + 4 * T].rearrange("a (r t) -> a r t", r=4).bitcast(I32)
             for cols in (slice(0, T // 8), slice(T // 8, T // 4)):
                 nc.sync.dma_start(out=planes[32 * quadrant : 32 * quadrant + 16, cols], in_=rows[:, :, cols])
-        for a in range(last):
-            load_words(a, slice(0, SPLIT))
-            load_weights(a + 1, 0, 2)
-            if a + 1 < last:
-                load_weights(a + 1, 2, 1)
-            load_words(a, slice(SPLIT, T))
-        load_words(last, slice(0, T))
-        load_weights(last, EARLY - 1, 2)
+        for a in range(LAST - 1):
+            load_weights(a + 1, 0, EARLY)
+            load_words(a)
+        load_words(LAST - 1, slice(0, T // 2))
+        load_weights(LAST, 0, EARLY - 1)
+        load_words(LAST - 1, slice(T // 2, T))
+        load_words(LAST)
         with nc.allow_non_contiguous_dma(reason="512 bias values, one to a partition"):
             nc.sync.dma_start(out=bias[:], in_=b.rearrange("(m p) -> p m", p=P))
-        for a in range(last):
+        load_weights(LAST, EARLY - 1, 2)
+        for a in range(LAST):
             load_weights(a, EARLY, 1)
 
-        interleaved = "p (c i j) -> p c j i"
-        WIDE = M_TILE * PACK
-        parts = {}
         codes = {}
 
-        def interleave(a, first, pool, name):
-            raw, count = raws[(a, first)]
-            upper = pool.tile([P, count * WIDE], BF16, name=name, align_bytes=ALIGN)
-            sixteens = raw[:].rearrange("p j n -> p (j n)").bitcast(BF16)
-            sixteens = sixteens.rearrange("p (j c i e) -> p c j i e", j=PACK, i=RUN, e=2)
-            nc.scalar.copy(out=upper[:].rearrange(interleaved, j=PACK, i=RUN), in_=sixteens[:, :, :, :, 1])
-            return upper
-
-        def mask(a, first, upper, start, count):
-            part = stage.tile([P, 2, count * WIDE], BF16, name="part%d" % count, align_bytes=ALIGN)
-            nc.vector.tensor_scalar(
-                out=part[:, 0].bitcast(I32),
-                in0=upper[:, start * WIDE : (start + count) * WIDE].bitcast(I32),
-                scalar1=HI_MASK,
-                scalar2=None,
-                op0=bitwise_and,
-            )
-            parts[(a, first + start)] = (part, raws[(a, first)][0][:, :, start * M_TILE : (start + count) * M_TILE], count)
-
-        def subtract_hi(a, m, engine):
-            part, raw, count = parts[(a, m)]
-            engine.tensor_tensor(
-                out=part[:, 1].rearrange(interleaved, j=PACK, i=RUN),
-                in0=raw.rearrange("p j (c i) -> p c j i", i=RUN),
-                in1=part[:, 0].rearrange(interleaved, j=PACK, i=RUN),
-                op=subtract,
-            )
-
-        def subtract_woven(a, m):
-            part, raw, count = parts[(a, m)]
-            woven = stage.tile([P, count * WIDE], F32, name="woven%d" % count, align_bytes=ALIGN, bufs=2)
-            nc.scalar.copy(out=woven[:].rearrange("p (n j) -> p n j", j=PACK), in_=raw.rearrange("p j n -> p n j"))
-            nc.gpsimd.tensor_tensor(out=part[:, 1], in0=woven[:], in1=part[:, 0], op=subtract)
-
-        def quantize(a, m):
-            part, raw, count = parts[(a, m)]
-            width = 2 * count * M_TILE
-            code = keep.tile([P, width], U32, name="code_%d_%d" % (a, m), align_bytes=ALIGN)
-            scale = keep.tile([P, width], U8, name="scale_%d_%d" % (a, m), align_bytes=ALIGN)
-            nc.vector.quantize_mx(out=code[:].bitcast(FP8X4), scales=scale[:], in_=part[:].rearrange("p s e -> p (s e)"))
-            for half in range(2):
-                for g in range(count):
-                    codes[(a, m + g, half)] = (code, scale, (half * count + g) * M_TILE)
-
-        def quantize_part(a, m, count, half, values):
+        def quantize(a, first, count, part, values, name=None):
             width = count * M_TILE
-            code = keep.tile([P, width], U32, name="late_code%d" % half, align_bytes=ALIGN)
-            scale = keep.tile([P, width], U8, name="late_scale%d" % half, align_bytes=ALIGN)
+            code = keep.tile([P, width], U32, name=name or "code_%d_%d_%d" % (a, first, part), align_bytes=ALIGN)
+            scale = keep.tile([P, width], U8, name="scale_%d_%d_%d" % (a, first, part), align_bytes=ALIGN)
             nc.vector.quantize_mx(out=code[:].bitcast(FP8X4), scales=scale[:], in_=values)
             for g in range(count):
-                codes[(a, m + g, half)] = (code, scale, g * M_TILE)
+                codes[(a, first + g, part)] = (code, scale, slice(g * M_TILE, (g + 1) * M_TILE))
+
+        def take_upper(a, first, upper):
+            sixteens = raws[(a, first)][:].rearrange("p j n -> p (j n)").bitcast(BF16)
+            sixteens = sixteens.rearrange("p (j c i e) -> p c j i e", j=PACK, i=RUN, e=2)
+            nc.scalar.copy(out=upper.rearrange(interleaved, j=PACK, i=RUN), in_=sixteens[:, :, :, :, 1])
+
+        def mask(upper, hi):
+            nc.vector.tensor_scalar(
+                out=hi.bitcast(I32), in0=upper.bitcast(I32), scalar1=HI_MASK, scalar2=None, op0=mybir.AluOpType.bitwise_and
+            )
+
+        def early_hi_and_lo(a, count):
+            upper = stage.tile([P, count * WIDE], BF16, name="upper", align_bytes=ALIGN)
+            hi = stage.tile([P, count * WIDE], BF16, name="hi", align_bytes=ALIGN)
+            lo = keep.tile([P, count * WIDE], BF16, name="lo%d" % a, align_bytes=ALIGN)
+            woven = keep.tile([P, count * WIDE], F32, name="woven%d" % a, align_bytes=ALIGN)
+            take_upper(a, 0, upper[:])
+            mask(upper[:], hi[:])
+            nc.scalar.copy(out=woven[:].rearrange("p (n j) -> p n j", j=PACK), in_=raws[(a, 0)][:].rearrange("p j n -> p n j"))
+            nc.gpsimd.tensor_tensor(out=lo[:], in0=woven[:], in1=hi[:], op=mybir.AluOpType.subtract)
+            return hi, lo
+
+        def late_lo(a, first, hi, lo):
+            nc.vector.tensor_tensor(
+                out=lo.rearrange(interleaved, j=PACK, i=RUN),
+                in0=raws[(a, first)][:].rearrange("p j (c i) -> p c j i", i=RUN),
+                in1=hi.rearrange(interleaved, j=PACK, i=RUN),
+                op=mybir.AluOpType.subtract,
+            )
 
         picked_planes = {}
         picked = {}
 
-        def list_part(n):
-            return offsets[:, n * N_TILE // LIST_ROWS : (n + 1) * N_TILE // LIST_ROWS]
+        def list_part(left, width):
+            return offsets[:, left // LIST_ROWS : (left + width) // LIST_ROWS]
 
         def gather_scales(n, name):
             picked_planes[n] = keep.tile([P, N_TILE], U8, name=name, align_bytes=ALIGN)
-            nc.vector.tensor_copy(out=picked_planes[n][:], in_=planes[:].bitcast(U8).indirect(list_part(n)))
+            nc.vector.tensor_copy(out=picked_planes[n][:], in_=planes[:].bitcast(U8).indirect(list_part(n * N_TILE, N_TILE)))
 
-        def gather_words(a, n, name):
-            picked[(a, n)] = keep.tile([P, N_TILE], U32, name=name, align_bytes=ALIGN)
-            nc.vector.tensor_copy(out=picked[(a, n)][:], in_=words[a][:].bitcast(U32).indirect(list_part(n)))
+        def gather_words(a, n, left=0, width=N_TILE, name=None):
+            if left == 0:
+                picked[(a, n)] = keep.tile([P, N_TILE], U32, name=name or "picked_%d_%d" % (a, n), align_bytes=ALIGN)
+            window = words[a][:].bitcast(U32)
+            nc.vector.tensor_copy(out=picked[(a, n)][:, left : left + width], in_=window.indirect(list_part(n * N_TILE + left, width)))
 
         sums = {}
-        bank_of = list(range(BANKS)) + [0, 1, 3, 4, 6, 7, 2, 5, 0, 6]
+        free_banks = list(range(BANKS))
 
-        def multiply(m, n, a, order, left=0, width=N_TILE, which=(0, 1)):
-            if (m, n, left) not in sums:
-                sums[(m, n, left)] = psum.tile([M_TILE, width], F32, name="acc%d" % bank_of[len(sums)])
-            for part in which:
-                code, scale, first = codes[(a, m, part)]
-                channels = slice(first, first + M_TILE)
-                nc.tensor.matmul_mx(
-                    out=sums[(m, n, left)][:],
-                    lhsT=code[:, channels].bitcast(FP8X4),
-                    lhsT_scale=scale[:, channels],
-                    rhs=picked[(a, n)][:, left : left + width].bitcast(FP8X4),
-                    rhs_scale=picked_planes[n][4 * a : P, left : left + width],
-                    start=(a == order[0] and part == 0),
-                    stop=(a == order[-1] and part == 1),
-                )
-            if a == order[-1] and which[-1] == 1:
-                done = outs.tile([M_TILE, width], F32, name="done")
-                nc.scalar.activation(out=done[:], in_=sums[(m, n, left)][:], func=silu, bias=bias[:, m : m + 1])
-                rows = slice(m * M_TILE, (m + 1) * M_TILE)
-                queue = nc.scalar if width < N_TILE // 2 and left + width == N_TILE else nc.sync
-                queue.dma_start(out=out[rows, n * N_TILE + left : n * N_TILE + left + width], in_=done[:])
+        def passes(key, m, n, a, part, left, width, origin, start, stop):
+            code, scale, channels = codes[(a, m, part)]
+            nc.tensor.matmul_mx(
+                out=sums[key][0][:, left - origin : left - origin + width],
+                lhsT=code[:, channels].bitcast(FP8X4),
+                lhsT_scale=scale[:, channels],
+                rhs=picked[(a, n)][:, left : left + width].bitcast(FP8X4),
+                rhs_scale=picked_planes[n][4 * a : P, left : left + width],
+                start=start,
+                stop=stop,
+            )
 
-        upward = list(range(PASSES))
+        def multiply(m, n, a, parts=(0, 1), left=0, width=N_TILE, origin=0, extent=N_TILE, closes=False):
+            key = (m, n, origin)
+            opens = key not in sums
+            if opens:
+                bank = free_banks.pop(0)
+                sums[key] = (psum.tile([M_TILE, extent], F32, name="acc%d" % bank), bank)
+            for part in parts:
+                passes(key, m, n, a, part, left, width, origin, opens and part == parts[0], closes and part == parts[-1])
+            if closes:
+                done = outs.tile([M_TILE, extent], F32, name="done")
+                nc.scalar.activation(out=done[:], in_=sums[key][0][:], func=silu, bias=bias[:, m : m + 1])
+                queue = nc.scalar if origin + extent == N_TILE and extent < N_HALF else nc.sync
+                cols = slice(n * N_TILE + origin, n * N_TILE + origin + extent)
+                queue.dma_start(out=out[m * M_TILE : (m + 1) * M_TILE, cols], in_=done[:])
+                free_banks.append(sums[key][1])
+
         first_sums = [(m, n) for n in range(EARLY) for m in range(EARLY)][:BANKS]
+        halves = (0, N_HALF)
 
-        mask(0, 0, interleave(0, 0, stage, "upper"), 0, 2)
-        mask(0, 2, interleave(0, 2, stage, "upper"), 0, 1)
-        subtract_woven(0, 0)
-        subtract_woven(0, 2)
+        hi, lo = early_hi_and_lo(0, EARLY)
+        quantize(0, 0, EARLY, 0, hi[:])
         for n in range(EARLY):
             gather_scales(n, "picked_planes%d" % n)
-        quantize(0, 0)
-        quantize(0, 2)
-        for a in range(last):
-            mask(a + 1, 0, interleave(a + 1, 0, stage, "upper"), 0, 2)
-            if a + 1 < last:
-                mask(a + 1, 2, interleave(a + 1, 2, stage, "upper"), 0, 1)
-            subtract_woven(a + 1, 0)
-            if a + 1 < last:
-                subtract_woven(a + 1, 2)
-            for n in range(EARLY):
-                gather_words(a, n, "picked_%d_%d" % (a, n))
-            quantize(a + 1, 0)
-            if a + 1 < last:
-                quantize(a + 1, 2)
-            for m, n in first_sums:
-                multiply(m, n, a, upward)
-        for n in range(N_TILES):
-            gather_words(last, n, "picked_%d_%d" % (last, n))
-        upper = interleave(last, EARLY - 1, stage, "upper")
+        quantize(0, 0, EARLY, 1, lo[:])
+        for a in range(LAST):
+            count = EARLY if a + 1 < LAST else EARLY - 1
+            hi, lo = early_hi_and_lo(a + 1, count)
+            for left in halves:
+                gather_words(a, 0, left, N_HALF)
+            for n in range(1, EARLY):
+                gather_words(a, n)
+            quantize(a + 1, 0, count, 0, hi[:], "woven%d" % (a + 1))
+            quantize(a + 1, 0, count, 1, lo[:])
+            for left in halves:
+                for m in range(EARLY):
+                    multiply(m, 0, a, left=left, width=N_HALF)
+            for m, n in first_sums[EARLY:]:
+                multiply(m, n, a)
+        upper = stage.tile([P, 2 * WIDE], BF16, name="upper", align_bytes=ALIGN)
+        take_upper(LAST, EARLY - 1, upper[:])
+        for n in range(EARLY - 1):
+            for left in halves:
+                gather_words(LAST, n, left, N_HALF)
+                for m in range(EARLY - 1):
+                    multiply(m, n, LAST, left=left, width=N_HALF, closes=left > 0)
+        gather_words(LAST, EARLY - 1)
+        for a in range(LAST):
+            multiply(EARLY - 1, EARLY - 1, a)
+        for m in range(EARLY - 1):
+            multiply(m, EARLY - 1, LAST, closes=True)
         hi = keep.tile([P, 2 * WIDE], BF16, name="late_hi", align_bytes=ALIGN)
-        lo = keep.tile([P, 2 * WIDE], BF16, name="shared%d" % last, align_bytes=ALIGN)
-        nc.vector.tensor_scalar(
-            out=hi[:].bitcast(I32), in0=upper[:].bitcast(I32), scalar1=HI_MASK, scalar2=None, op0=bitwise_and
-        )
-        quantize_part(last, EARLY - 1, 2, 0, hi[:])
-        nc.vector.tensor_tensor(
-            out=lo[:].rearrange(interleaved, j=PACK, i=RUN),
-            in0=raws[(last, EARLY - 1)][0][:].rearrange("p j (c i) -> p c j i", i=RUN),
-            in1=hi[:].rearrange(interleaved, j=PACK, i=RUN),
-            op=subtract,
-        )
-        quantize_part(last, EARLY - 1, 2, 1, lo[:])
-        gather_scales(EARLY, "shared%d" % last)
-        for m, n in first_sums:
-            if m < EARLY - 1:
-                multiply(m, n, last, upward)
-        for a in range(last):
-            mask(a, EARLY, interleave(a, EARLY, keep, "shared%d" % a), 0, 1)
-            gather_words(a, EARLY, "shared%d" % a)
-            subtract_hi(a, EARLY, nc.vector)
-            quantize(a, EARLY)
-        for a in range(last):
-            multiply(EARLY - 1, EARLY - 1, a, upward)
-        turned = [last] + upward[:last]
+        lo = keep.tile([P, 2 * WIDE], BF16, name="shared%d" % LAST, align_bytes=ALIGN)
+        mask(upper[:], hi[:])
+        quantize(LAST, EARLY - 1, 2, 0, hi[:])
+        late_lo(LAST, EARLY - 1, hi[:], lo[:])
+        quantize(LAST, EARLY - 1, 2, 1, lo[:])
+        gather_words(LAST, EARLY, name="shared%d" % LAST)
+        gather_scales(EARLY, "late_hi")
+        for a in range(LAST):
+            upper = keep.tile([P, WIDE], BF16, name="shared%d" % a, align_bytes=ALIGN)
+            both = stage.tile([P, 2, WIDE], BF16, name="both", align_bytes=ALIGN)
+            take_upper(a, EARLY, upper[:])
+            mask(upper[:], both[:, 0])
+            gather_words(a, EARLY, name="shared%d" % a)
+            late_lo(a, EARLY, both[:, 0], both[:, 1])
+            code = keep.tile([P, 2 * M_TILE], U32, name="code_late%d" % a, align_bytes=ALIGN)
+            scale = keep.tile([P, 2 * M_TILE], U8, name="scale_late%d" % a, align_bytes=ALIGN)
+            nc.vector.quantize_mx(out=code[:].bitcast(FP8X4), scales=scale[:], in_=both[:].rearrange("p s e -> p (s e)"))
+            for part in range(2):
+                codes[(a, EARLY, part)] = (code, scale, slice(part * M_TILE, (part + 1) * M_TILE))
         for part in range(2):
-            for n in range(EARLY):
-                multiply(EARLY - 1, n, last, upward, which=(part,))
-            for n in range(EARLY):
-                multiply(EARLY, n, last, turned, which=(part,))
-        for a in turned:
-            for m in range(EARLY):
-                multiply(m, EARLY, a, turned)
-            if a != last:
+            for m in (EARLY - 1, EARLY):
                 for n in range(EARLY):
-                    multiply(EARLY, n, a, turned)
-        for left, width in [(0, N_TILE // 2), (N_TILE // 2, N_TILE // 4), (3 * N_TILE // 4, N_TILE // 4)]:
-            for a in upward:
-                multiply(EARLY, EARLY, a, upward, left, width)
+                    multiply(m, n, LAST, parts=(part,), closes=(m < EARLY and part == 1))
+        for a in [LAST] + list(range(LAST)):
+            for m in range(EARLY):
+                multiply(m, EARLY, a, closes=a == LAST - 1)
+            if a != LAST:
+                for n in range(EARLY):
+                    multiply(EARLY, n, a, closes=a == LAST - 1)
+        for origin, extent in [(0, N_HALF), (N_HALF, N_HALF // 2), (3 * N_HALF // 2, N_HALF // 2)]:
+            for a in range(PASSES):
+                multiply(EARLY, EARLY, a, left=origin, width=extent, origin=origin, extent=extent, closes=a == LAST)

@@ -171,7 +171,7 @@ def tile_list_tabw_hl_silu_kernel(tc, tab, w, b, offs, out):
 
         hi, lo = early_hi_and_lo(0, EARLY)
         quantize(0, 0, EARLY, 0, hi[:])
-        for n in range(EARLY):
+        for n in range(N_TILES):
             gather_scales(n, "picked_planes%d" % n)
         quantize(0, 0, EARLY, 1, lo[:])
         for a in range(LAST):
@@ -207,7 +207,6 @@ def tile_list_tabw_hl_silu_kernel(tc, tab, w, b, offs, out):
         late_lo(LAST, EARLY - 1, hi[:], lo[:])
         quantize(LAST, EARLY - 1, 2, 1, lo[:])
         gather_words(LAST, EARLY, name="shared%d" % LAST)
-        gather_scales(EARLY, "late_hi")
         for a in range(LAST):
             upper = keep.tile([P, WIDE], BF16, name="shared%d" % a, align_bytes=ALIGN)
             both = stage.tile([P, 2, WIDE], BF16, name="both", align_bytes=ALIGN)

@@ -29,6 +29,7 @@ ALIGN = 64
 HI_MASK = 0xFFF0FFF0 - 2**32
 RUN = 4
 EARLY = 3
+SPLIT = 1536
 WIDE = M_TILE * PACK
 
 
@@ -70,9 +71,9 @@ def tile_list_tabw_hl_silu_kernel(tc, tab, w, b, offs, out):
         for a in range(LAST - 1):
             load_weights(a + 1, 0, EARLY)
             load_words(a)
-        load_words(LAST - 1, slice(0, T // 2))
+        load_words(LAST - 1, slice(0, SPLIT))
         load_weights(LAST, 0, EARLY - 1)
-        load_words(LAST - 1, slice(T // 2, T))
+        load_words(LAST - 1, slice(SPLIT, T))
         load_words(LAST)
         with nc.allow_non_contiguous_dma(reason="512 bias values, one to a partition"):
             nc.sync.dma_start(out=bias[:], in_=b.rearrange("(m p) -> p m", p=P))
@@ -103,10 +104,12 @@ def tile_list_tabw_hl_silu_kernel(tc, tab, w, b, offs, out):
         def early_hi_and_lo(a, count):
             upper = stage.tile([P, count * WIDE], BF16, name="upper", align_bytes=ALIGN)
             hi = stage.tile([P, count * WIDE], BF16, name="hi", align_bytes=ALIGN)
-            lo = keep.tile([P, count * WIDE], BF16, name="lo%d" % a, align_bytes=ALIGN)
+            lo = hi if a > 1 else keep.tile([P, count * WIDE], BF16, name="lo%d" % a, align_bytes=ALIGN)
             woven = keep.tile([P, count * WIDE], F32, name="woven%d" % a, align_bytes=ALIGN)
             take_upper(a, 0, upper[:])
             mask(upper[:], hi[:])
+            if a > 1:
+                quantize(a, 0, count, 0, hi[:])
             nc.scalar.copy(out=woven[:].rearrange("p (n j) -> p n j", j=PACK), in_=raws[(a, 0)][:].rearrange("p j n -> p n j"))
             nc.gpsimd.tensor_tensor(out=lo[:], in0=woven[:], in1=hi[:], op=mybir.AluOpType.subtract)
             return hi, lo
@@ -171,7 +174,7 @@ def tile_list_tabw_hl_silu_kernel(tc, tab, w, b, offs, out):
 
         hi, lo = early_hi_and_lo(0, EARLY)
         quantize(0, 0, EARLY, 0, hi[:])
-        for n in range(N_TILES):
+        for n in range(EARLY):
             gather_scales(n, "picked_planes%d" % n)
         quantize(0, 0, EARLY, 1, lo[:])
         for a in range(LAST):
@@ -181,7 +184,8 @@ def tile_list_tabw_hl_silu_kernel(tc, tab, w, b, offs, out):
                 gather_words(a, 0, left, N_HALF)
             for n in range(1, EARLY):
                 gather_words(a, n)
-            quantize(a + 1, 0, count, 0, hi[:], "woven%d" % (a + 1))
+            if a == 0:
+                quantize(a + 1, 0, count, 0, hi[:], "woven%d" % (a + 1))
             quantize(a + 1, 0, count, 1, lo[:])
             for left in halves:
                 for m in range(EARLY):
@@ -207,6 +211,7 @@ def tile_list_tabw_hl_silu_kernel(tc, tab, w, b, offs, out):
         late_lo(LAST, EARLY - 1, hi[:], lo[:])
         quantize(LAST, EARLY - 1, 2, 1, lo[:])
         gather_words(LAST, EARLY, name="shared%d" % LAST)
+        gather_scales(EARLY, "late_hi")
         for a in range(LAST):
             upper = keep.tile([P, WIDE], BF16, name="shared%d" % a, align_bytes=ALIGN)
             both = stage.tile([P, 2, WIDE], BF16, name="both", align_bytes=ALIGN)

@@ -60,14 +60,14 @@ def tile_list_tabw_hl_silu_kernel(tc, tab, w, b, offs, out):
             rows = tab[a, 0 : K_PASS * T].rearrange("(p t) -> p t", p=P).bitcast(I32)
             nc.sync.dma_start(out=words[a][:, cols], in_=rows[:, cols])
 
-        nc.sync.dma_start(offsets[:], offs)
         nc.vector.memset(planes[:], 0)
         load_weights(0, 0, EARLY)
         for quadrant in (2, 3, 0, 1):
             first = K_PASS * T + 4 * quadrant * T
             rows = tab[:, first : first + 4 * T].rearrange("a (r t) -> a r t", r=4).bitcast(I32)
-            for cols in (slice(0, T // 8), slice(T // 8, T // 4)):
+            for cols in (slice(0, T // 8), slice(T // 8, T // 4)) if quadrant >= 2 else (slice(0, T // 4),):
                 nc.sync.dma_start(out=planes[32 * quadrant : 32 * quadrant + 16, cols], in_=rows[:, :, cols])
+        nc.sync.dma_start(offsets[:], offs)
         for a in range(LAST - 1):
             load_weights(a + 1, 0, EARLY)
             load_words(a)

@@ -25,7 +25,10 @@ N_HALF = N_TILE // 2
 N_TILES = S // N_TILE
 BANKS = 8
 LIST_ROWS = 16
-ALIGN = 64
+ALIGN = 256
+MOVING_SCALES_AT = 64
+STATIONARY_CODES_AT = 128
+STATIONARY_SCALES_AT = 192
 HI_MASK = 0xFFF0FFF0 - 2**32
 RUN = 4
 EARLY = 3
@@ -83,11 +86,15 @@ def tile_list_tabw_hl_silu_kernel(tc, tab, w, b, offs, out):
 
         codes = {}
 
+        def codes_and_scales(width, name, shared=None):
+            code = keep.tile([P, STATIONARY_CODES_AT // 4 + width], U32, name=shared or "code_" + name, align_bytes=ALIGN)
+            scale = keep.tile([P, STATIONARY_SCALES_AT + width], U8, name="scale_" + name, align_bytes=ALIGN)
+            return code[:, STATIONARY_CODES_AT // 4 :], scale[:, STATIONARY_SCALES_AT:]
+
         def quantize(a, first, count, part, values, name=None):
             width = count * M_TILE
-            code = keep.tile([P, width], U32, name=name or "code_%d_%d_%d" % (a, first, part), align_bytes=ALIGN)
-            scale = keep.tile([P, width], U8, name="scale_%d_%d_%d" % (a, first, part), align_bytes=ALIGN)
-            nc.vector.quantize_mx(out=code[:].bitcast(FP8X4), scales=scale[:], in_=values)
+            code, scale = codes_and_scales(width, "%d_%d_%d" % (a, first, part), name)
+            nc.vector.quantize_mx(out=code.bitcast(FP8X4), scales=scale, in_=values)
             for g in range(count):
                 codes[(a, first + g, part)] = (code, scale, slice(g * M_TILE, (g + 1) * M_TILE))
 
@@ -129,8 +136,9 @@ def tile_list_tabw_hl_silu_kernel(tc, tab, w, b, offs, out):
             return offsets[:, left // LIST_ROWS : (left + width) // LIST_ROWS]
 
         def gather_scales(n, name):
-            picked_planes[n] = keep.tile([P, N_TILE], U8, name=name, align_bytes=ALIGN)
-            nc.vector.tensor_copy(out=picked_planes[n][:], in_=planes[:].bitcast(U8).indirect(list_part(n * N_TILE, N_TILE)))
+            tile = keep.tile([P, MOVING_SCALES_AT + N_TILE], U8, name=name, align_bytes=ALIGN)
+            picked_planes[n] = tile[:, MOVING_SCALES_AT:]
+            nc.vector.tensor_copy(out=picked_planes[n], in_=planes[:].bitcast(U8).indirect(list_part(n * N_TILE, N_TILE)))
 
         def gather_words(a, n, left=0, width=N_TILE, name=None):
             if left == 0:
@@ -169,7 +177,6 @@ def tile_list_tabw_hl_silu_kernel(tc, tab, w, b, offs, out):
                 queue.dma_start(out=out[m * M_TILE : (m + 1) * M_TILE, cols], in_=done[:])
                 free_banks.append(sums[key][1])
 
-        first_sums = [(m, n) for n in range(EARLY) for m in range(EARLY)][:BANKS]
         halves = (0, N_HALF)
 
         hi, lo = early_hi_and_lo(0, EARLY)
@@ -180,18 +187,19 @@ def tile_list_tabw_hl_silu_kernel(tc, tab, w, b, offs, out):
         for a in range(LAST):
             count = EARLY if a + 1 < LAST else EARLY - 1
             hi, lo = early_hi_and_lo(a + 1, count)
-            for left in halves:
-                gather_words(a, 0, left, N_HALF)
-            for n in range(1, EARLY):
-                gather_words(a, n)
+            for n in range(EARLY - 1):
+                for left in halves:
+                    gather_words(a, n, left, N_HALF)
+            gather_words(a, EARLY - 1)
             if a == 0:
                 quantize(a + 1, 0, count, 0, hi[:], "woven%d" % (a + 1))
             quantize(a + 1, 0, count, 1, lo[:])
-            for left in halves:
-                for m in range(EARLY):
-                    multiply(m, 0, a, left=left, width=N_HALF)
-            for m, n in first_sums[EARLY:]:
-                multiply(m, n, a)
+            for n in range(EARLY - 1):
+                for left in halves:
+                    for m in range(EARLY):
+                        multiply(m, n, a, left=left, width=N_HALF)
+            for m in range(EARLY - 1):
+                multiply(m, EARLY - 1, a)
         upper = stage.tile([P, 2 * WIDE], BF16, name="upper", align_bytes=ALIGN)
         take_upper(LAST, EARLY - 1, upper[:])
         for n in range(EARLY - 1):
@@ -219,9 +227,8 @@ def tile_list_tabw_hl_silu_kernel(tc, tab, w, b, offs, out):
             mask(upper[:], both[:, 0])
             gather_words(a, EARLY, name="shared%d" % a)
             late_lo(a, EARLY, both[:, 0], both[:, 1])
-            code = keep.tile([P, 2 * M_TILE], U32, name="code_late%d" % a, align_bytes=ALIGN)
-            scale = keep.tile([P, 2 * M_TILE], U8, name="scale_late%d" % a, align_bytes=ALIGN)
-            nc.vector.quantize_mx(out=code[:].bitcast(FP8X4), scales=scale[:], in_=both[:].rearrange("p s e -> p (s e)"))
+            code, scale = codes_and_scales(2 * M_TILE, "late%d" % a)
+            nc.vector.quantize_mx(out=code.bitcast(FP8X4), scales=scale, in_=both[:].rearrange("p s e -> p (s e)"))
             for part in range(2):
                 codes[(a, EARLY, part)] = (code, scale, slice(part * M_TILE, (part + 1) * M_TILE))
         for part in range(2):

@@ -187,17 +187,18 @@ def tile_list_tabw_hl_silu_kernel(tc, tab, w, b, offs, out):
         for a in range(LAST):
             count = EARLY if a + 1 < LAST else EARLY - 1
             hi, lo = early_hi_and_lo(a + 1, count)
-            for n in range(EARLY - 1):
-                for left in halves:
-                    gather_words(a, n, left, N_HALF)
-            gather_words(a, EARLY - 1)
+            for left in halves:
+                gather_words(a, 0, left, N_HALF)
+            for n in range(1, EARLY):
+                gather_words(a, n)
             if a == 0:
                 quantize(a + 1, 0, count, 0, hi[:], "woven%d" % (a + 1))
             quantize(a + 1, 0, count, 1, lo[:])
-            for n in range(EARLY - 1):
-                for left in halves:
-                    for m in range(EARLY):
-                        multiply(m, n, a, left=left, width=N_HALF)
+            for left in halves:
+                for m in range(EARLY):
+                    multiply(m, 0, a, left=left, width=N_HALF)
+            for m in range(EARLY):
+                multiply(m, 1, a)
             for m in range(EARLY - 1):
                 multiply(m, EARLY - 1, a)
         upper = stage.tile([P, 2 * WIDE], BF16, name="upper", align_bytes=ALIGN)

@@ -27,8 +27,8 @@ BANKS = 8
 LIST_ROWS = 16
 ALIGN = 256
 MOVING_SCALES_AT = 64
-STATIONARY_CODES_AT = 128
-STATIONARY_SCALES_AT = 192
+STATIONARY_CODES_AT = 192
+STATIONARY_SCALES_AT = 128
 HI_MASK = 0xFFF0FFF0 - 2**32
 RUN = 4
 EARLY = 3

@@ -170,7 +170,7 @@ def tile_list_tabw_hl_silu_kernel(tc, tab, w, b, offs, out):
             for part in parts:
                 passes(key, m, n, a, part, left, width, origin, opens and part == parts[0], closes and part == parts[-1])
             if closes:
-                done = outs.tile([M_TILE, extent], F32, name="done")
+                done = outs.tile([M_TILE, extent], F32, name="done", align_bytes=ALIGN)
                 nc.scalar.activation(out=done[:], in_=sums[key][0][:], func=silu, bias=bias[:, m : m + 1])
                 queue = nc.scalar if origin + extent == N_TILE and extent < N_HALF else nc.sync
                 cols = slice(n * N_TILE + origin, n * N_TILE + origin + extent)
@@ -187,18 +187,18 @@ def tile_list_tabw_hl_silu_kernel(tc, tab, w, b, offs, out):
         for a in range(LAST):
             count = EARLY if a + 1 < LAST else EARLY - 1
             hi, lo = early_hi_and_lo(a + 1, count)
-            for left in halves:
-                gather_words(a, 0, left, N_HALF)
-            for n in range(1, EARLY):
-                gather_words(a, n)
+            pieces = [(left, N_HALF) for left in halves] if a == LAST - 1 else [(0, N_TILE)]
+            for n in range(EARLY - 1):
+                for left, width in pieces:
+                    gather_words(a, n, left, width)
+            gather_words(a, EARLY - 1)
             if a == 0:
                 quantize(a + 1, 0, count, 0, hi[:], "woven%d" % (a + 1))
             quantize(a + 1, 0, count, 1, lo[:])
-            for left in halves:
-                for m in range(EARLY):
-                    multiply(m, 0, a, left=left, width=N_HALF)
-            for m in range(EARLY):
-                multiply(m, 1, a)
+            for n in range(EARLY - 1):
+                for left, width in pieces:
+                    for m in range(EARLY):
+                        multiply(m, n, a, left=left, width=width)
             for m in range(EARLY - 1):
                 multiply(m, EARLY - 1, a)
         upper = stage.tile([P, 2 * WIDE], BF16, name="upper", align_bytes=ALIGN)

@@ -26,9 +26,9 @@ N_TILES = S // N_TILE
 BANKS = 8
 LIST_ROWS = 16
 ALIGN = 256
-MOVING_SCALES_AT = 64
-STATIONARY_CODES_AT = 192
-STATIONARY_SCALES_AT = 128
+MOVING_SCALES_AT = 0
+STATIONARY_CODES_AT = 0
+STATIONARY_SCALES_AT = 0
 HI_MASK = 0xFFF0FFF0 - 2**32
 RUN = 4
 EARLY = 3

from contextlib import ExitStack

import concourse.mybir as mybir

K, M, T, S = 2048, 512, 4096, 2048
FLOPS = 2 * 2 * K * M * S

F32 = mybir.dt.float32
BF16 = mybir.dt.bfloat16
I32 = mybir.dt.int32
U32 = mybir.dt.uint32
U16 = mybir.dt.uint16
U8 = mybir.dt.uint8
FP8X4 = mybir.dt.float8_e4m3fn_x4

P = 128
PACK = 4
K_PASS = P * PACK
PASSES = K // K_PASS
LAST = PASSES - 1
M_TILE = 128
M_TILES = M // M_TILE
N_TILE = 512
N_HALF = N_TILE // 2
N_TILES = S // N_TILE
BANKS = 8
LIST_ROWS = 16
ALIGN = 256
MOVING_SCALES_AT = 0
STATIONARY_CODES_AT = 0
STATIONARY_SCALES_AT = 0
HI_MASK = 0xFFF0FFF0 - 2**32
RUN = 4
EARLY = 3
SPLIT = 1536
WIDE = M_TILE * PACK


def tile_list_tabw_hl_silu_kernel(tc, tab, w, b, offs, out):
    nc = tc.nc
    silu = mybir.ActivationFunctionType.Silu
    interleaved = "p (c i j) -> p c j i"

    with ExitStack() as ctx:
        keep = ctx.enter_context(tc.tile_pool(name="keep", bufs=1))
        stage = ctx.enter_context(tc.tile_pool(name="stage", bufs=2))
        outs = ctx.enter_context(tc.tile_pool(name="outs", bufs=BANKS))
        psum = ctx.enter_context(tc.psum_pool(name="psum", bufs=1))

        offsets = keep.tile([P, S // LIST_ROWS], U16, name="offsets")
        planes = keep.tile([P, T // 4], I32, name="planes", align_bytes=ALIGN)
        words = [keep.tile([P, T], I32, name="words%d" % a, align_bytes=ALIGN) for a in range(PASSES)]
        bias = keep.tile([P, M_TILES], F32, name="bias")
        raws = {}

        def load_weights(a, first, count):
            raw = keep.tile([P, PACK, count * M_TILE], F32, name="raw_%d_%d" % (a, first), align_bytes=ALIGN)
            rows = w[a * K_PASS : (a + 1) * K_PASS, first * M_TILE : (first + count) * M_TILE]
            nc.sync.dma_start(out=raw[:], in_=rows.rearrange("(p j) n -> p j n", j=PACK))
            raws[(a, first)] = raw

        def load_words(a, cols=slice(0, T)):
            rows = tab[a, 0 : K_PASS * T].rearrange("(p t) -> p t", p=P).bitcast(I32)
            nc.sync.dma_start(out=words[a][:, cols], in_=rows[:, cols])

        nc.vector.memset(planes[:], 0)
        load_weights(0, 0, EARLY)
        for quadrant in (2, 3, 0, 1):
            first = K_PASS * T + 4 * quadrant * T
            rows = tab[:, first : first + 4 * T].rearrange("a (r t) -> a r t", r=4).bitcast(I32)
            for cols in (slice(0, T // 8), slice(T // 8, T // 4)) if quadrant >= 2 else (slice(0, T // 4),):
                nc.sync.dma_start(out=planes[32 * quadrant : 32 * quadrant + 16, cols], in_=rows[:, :, cols])
        nc.sync.dma_start(offsets[:], offs)
        for a in range(LAST - 1):
            load_weights(a + 1, 0, EARLY)
            load_words(a)
        load_words(LAST - 1, slice(0, SPLIT))
        load_weights(LAST, 0, EARLY - 1)
        load_words(LAST - 1, slice(SPLIT, T))
        load_words(LAST)
        with nc.allow_non_contiguous_dma(reason="512 bias values, one to a partition"):
            nc.sync.dma_start(out=bias[:], in_=b.rearrange("(m p) -> p m", p=P))
        load_weights(LAST, EARLY - 1, 2)
        for a in range(LAST):
            load_weights(a, EARLY, 1)

        codes = {}

        def codes_and_scales(width, name, shared=None):
            code = keep.tile([P, STATIONARY_CODES_AT // 4 + width], U32, name=shared or "code_" + name, align_bytes=ALIGN)
            scale = keep.tile([P, STATIONARY_SCALES_AT + width], U8, name="scale_" + name, align_bytes=ALIGN)
            return code[:, STATIONARY_CODES_AT // 4 :], scale[:, STATIONARY_SCALES_AT:]

        def quantize(a, first, count, part, values, name=None):
            width = count * M_TILE
            code, scale = codes_and_scales(width, "%d_%d_%d" % (a, first, part), name)
            nc.vector.quantize_mx(out=code.bitcast(FP8X4), scales=scale, in_=values)
            for g in range(count):
                codes[(a, first + g, part)] = (code, scale, slice(g * M_TILE, (g + 1) * M_TILE))

        def take_upper(a, first, upper):
            sixteens = raws[(a, first)][:].rearrange("p j n -> p (j n)").bitcast(BF16)
            sixteens = sixteens.rearrange("p (j c i e) -> p c j i e", j=PACK, i=RUN, e=2)
            nc.scalar.copy(out=upper.rearrange(interleaved, j=PACK, i=RUN), in_=sixteens[:, :, :, :, 1])

        def mask(upper, hi):
            nc.vector.tensor_scalar(
                out=hi.bitcast(I32), in0=upper.bitcast(I32), scalar1=HI_MASK, scalar2=None, op0=mybir.AluOpType.bitwise_and
            )

        def early_hi_and_lo(a, count):
            upper = stage.tile([P, count * WIDE], BF16, name="upper", align_bytes=ALIGN)
            hi = stage.tile([P, count * WIDE], BF16, name="hi", align_bytes=ALIGN)
            lo = hi if a > 1 else keep.tile([P, count * WIDE], BF16, name="lo%d" % a, align_bytes=ALIGN)
            woven = keep.tile([P, count * WIDE], F32, name="woven%d" % a, align_bytes=ALIGN)
            take_upper(a, 0, upper[:])
            mask(upper[:], hi[:])
            if a > 1:
                quantize(a, 0, count, 0, hi[:])
            nc.scalar.copy(out=woven[:].rearrange("p (n j) -> p n j", j=PACK), in_=raws[(a, 0)][:].rearrange("p j n -> p n j"))
            nc.gpsimd.tensor_tensor(out=lo[:], in0=woven[:], in1=hi[:], op=mybir.AluOpType.subtract)
            return hi, lo

        def late_lo(a, first, hi, lo):
            nc.vector.tensor_tensor(
                out=lo.rearrange(interleaved, j=PACK, i=RUN),
                in0=raws[(a, first)][:].rearrange("p j (c i) -> p c j i", i=RUN),
                in1=hi.rearrange(interleaved, j=PACK, i=RUN),
                op=mybir.AluOpType.subtract,
            )

        picked_planes = {}
        picked = {}

        def list_part(left, width):
            return offsets[:, left // LIST_ROWS : (left + width) // LIST_ROWS]

        def gather_scales(n, name):
            tile = keep.tile([P, MOVING_SCALES_AT + N_TILE], U8, name=name, align_bytes=ALIGN)
            picked_planes[n] = tile[:, MOVING_SCALES_AT:]
            nc.vector.tensor_copy(out=picked_planes[n], in_=planes[:].bitcast(U8).indirect(list_part(n * N_TILE, N_TILE)))

        def gather_words(a, n, left=0, width=N_TILE, name=None):
            if left == 0:
                picked[(a, n)] = keep.tile([P, N_TILE], U32, name=name or "picked_%d_%d" % (a, n), align_bytes=ALIGN)
            window = words[a][:].bitcast(U32)
            nc.vector.tensor_copy(out=picked[(a, n)][:, left : left + width], in_=window.indirect(list_part(n * N_TILE + left, width)))

        sums = {}
        free_banks = list(range(BANKS))

        def passes(key, m, n, a, part, left, width, origin, start, stop):
            code, scale, channels = codes[(a, m, part)]
            nc.tensor.matmul_mx(
                out=sums[key][0][:, left - origin : left - origin + width],
                lhsT=code[:, channels].bitcast(FP8X4),
                lhsT_scale=scale[:, channels],
                rhs=picked[(a, n)][:, left : left + width].bitcast(FP8X4),
                rhs_scale=picked_planes[n][4 * a : P, left : left + width],
                start=start,
                stop=stop,
            )

        def multiply(m, n, a, parts=(0, 1), left=0, width=N_TILE, origin=0, extent=N_TILE, closes=False):
            key = (m, n, origin)
            opens = key not in sums
            if opens:
                bank = free_banks.pop(0)
                sums[key] = (psum.tile([M_TILE, extent], F32, name="acc%d" % bank), bank)
            for part in parts:
                passes(key, m, n, a, part, left, width, origin, opens and part == parts[0], closes and part == parts[-1])
            if closes:
                done = outs.tile([M_TILE, extent], F32, name="done", align_bytes=ALIGN)
                nc.scalar.activation(out=done[:], in_=sums[key][0][:], func=silu, bias=bias[:, m : m + 1])
                queue = nc.scalar if origin + extent == N_TILE and extent < N_HALF else nc.sync
                cols = slice(n * N_TILE + origin, n * N_TILE + origin + extent)
                queue.dma_start(out=out[m * M_TILE : (m + 1) * M_TILE, cols], in_=done[:])
                free_banks.append(sums[key][1])

        halves = (0, N_HALF)

        hi, lo = early_hi_and_lo(0, EARLY)
        quantize(0, 0, EARLY, 0, hi[:])
        for n in range(EARLY):
            gather_scales(n, "picked_planes%d" % n)
        quantize(0, 0, EARLY, 1, lo[:])
        for a in range(LAST):
            count = EARLY if a + 1 < LAST else EARLY - 1
            hi, lo = early_hi_and_lo(a + 1, count)
            pieces = [(left, N_HALF) for left in halves] if a == LAST - 1 else [(0, N_TILE)]
            for n in range(EARLY - 1):
                for left, width in pieces:
                    gather_words(a, n, left, width)
            gather_words(a, EARLY - 1)
            if a == 0:
                quantize(a + 1, 0, count, 0, hi[:], "woven%d" % (a + 1))
            quantize(a + 1, 0, count, 1, lo[:])
            for n in range(EARLY - 1):
                for left, width in pieces:
                    for m in range(EARLY):
                        multiply(m, n, a, left=left, width=width)
            for m in range(EARLY - 1):
                multiply(m, EARLY - 1, a)
        upper = stage.tile([P, 2 * WIDE], BF16, name="upper", align_bytes=ALIGN)
        take_upper(LAST, EARLY - 1, upper[:])
        for n in range(EARLY - 1):
            for left in halves:
                gather_words(LAST, n, left, N_HALF)
                for m in range(EARLY - 1):
                    multiply(m, n, LAST, left=left, width=N_HALF, closes=left > 0)
        gather_words(LAST, EARLY - 1)
        for a in range(LAST):
            multiply(EARLY - 1, EARLY - 1, a)
        for m in range(EARLY - 1):
            multiply(m, EARLY - 1, LAST, closes=True)
        hi = keep.tile([P, 2 * WIDE], BF16, name="late_hi", align_bytes=ALIGN)
        lo = keep.tile([P, 2 * WIDE], BF16, name="shared%d" % LAST, align_bytes=ALIGN)
        mask(upper[:], hi[:])
        quantize(LAST, EARLY - 1, 2, 0, hi[:])
        late_lo(LAST, EARLY - 1, hi[:], lo[:])
        quantize(LAST, EARLY - 1, 2, 1, lo[:])
        gather_words(LAST, EARLY, name="shared%d" % LAST)
        gather_scales(EARLY, "late_hi")
        for a in range(LAST):
            upper = keep.tile([P, WIDE], BF16, name="shared%d" % a, align_bytes=ALIGN)
            both = stage.tile([P, 2, WIDE], BF16, name="both", align_bytes=ALIGN)
            take_upper(a, EARLY, upper[:])
            mask(upper[:], both[:, 0])
            gather_words(a, EARLY, name="shared%d" % a)
            late_lo(a, EARLY, both[:, 0], both[:, 1])
            code, scale = codes_and_scales(2 * M_TILE, "late%d" % a)
            nc.vector.quantize_mx(out=code.bitcast(FP8X4), scales=scale, in_=both[:].rearrange("p s e -> p (s e)"))
            for part in range(2):
                codes[(a, EARLY, part)] = (code, scale, slice(part * M_TILE, (part + 1) * M_TILE))
        for part in range(2):
            for m in (EARLY - 1, EARLY):
                for n in range(EARLY):
                    multiply(m, n, LAST, parts=(part,), closes=(m < EARLY and part == 1))
        for a in [LAST] + list(range(LAST)):
            for m in range(EARLY):
                multiply(m, EARLY, a, closes=a == LAST - 1)
            if a != LAST:
                for n in range(EARLY):
                    multiply(EARLY, n, a, closes=a == LAST - 1)
        for origin, extent in [(0, N_HALF), (N_HALF, N_HALF // 2), (3 * N_HALF // 2, N_HALF // 2)]:
            for a in range(PASSES):
                multiply(EARLY, EARLY, a, left=origin, width=extent, origin=origin, extent=extent, closes=a == LAST)
